import numpy as np
import ml_dtypes


def mxq(x, axis, fmt="e4m3"):
    dtype, down = {"e4m3": (ml_dtypes.float8_e4m3fn, 7), "e5m2": (ml_dtypes.float8_e5m2, 14)}[fmt]
    v = np.moveaxis(np.asarray(x, np.float32).astype(ml_dtypes.bfloat16).astype(np.float64), axis, -1)
    blocks = v.reshape(v.shape[:-1] + (-1, 32))
    amax = np.abs(blocks).max(-1, keepdims=True)
    byte = np.maximum(np.where(amax > 0, np.frexp(amax)[1] - 1 + 127, 0) - down, 1)
    scale = np.exp2(byte - 127.0)
    codes = (blocks / scale).astype(np.float32).astype(dtype).astype(np.float64)
    return np.moveaxis((codes * scale).reshape(v.shape), -1, axis)


WIDE = False


def mx_kscale(k):
    if not WIDE:
        return np.ones(k)
    levels = np.array([10, -10, 5, -5, 0])
    if k % 512:
        return np.exp2(np.random.permutation(np.resize(levels, k // 32))).repeat(32)
    a = np.empty((k // 512, 16))
    for p in range(k // 512):
        a[p, :8] = np.random.permutation(np.resize(levels, 8))
        for g in range(8):
            far = levels[np.abs(levels - a[p, g]) >= 10]
            a[p, g + 8] = far[np.random.randint(len(far))]
    return np.exp2(a.ravel()).repeat(32)


BF16 = ml_dtypes.bfloat16


def bf(x):
    return np.asarray(x, np.float32).astype(BF16)


def f64(x):
    return np.asarray(x).astype(np.float64)

def planes(Y):
    n, m = Y.shape
    b = f64(bf(Y)).reshape(n // 32, 32, m)
    amax = np.abs(b).max(1)
    byte = np.clip(np.where(amax > 0, np.frexp(amax)[1] - 1 + 127 - 7, 1), 1, 254)
    codes = (b * np.exp2(127.0 - byte)[:, None, :]).reshape(n, m).astype(np.float32).astype(ml_dtypes.float8_e4m3fn).view(np.uint8)
    words = codes.reshape(n // 512, 128, 4, m).transpose(0, 1, 3, 2)
    return np.ascontiguousarray(words), np.ascontiguousarray(byte.astype(np.uint8).reshape(n // 512, 16, m))


R, T, L = 1536, 1024, 512
NOISE = 0.3
SPREAD = 0.8


def setup_inputs():
    rn = np.random.randn
    s = mx_kscale(T)
    h_re = bf(rn(R, T) / np.sqrt(2 * T) * s[None, :])
    h_im = bf(rn(R, T) / np.sqrt(2 * T) * s[None, :])
    x_re = bf(rn(T, L) / s[:, None])
    x_im = bf(rn(T, L) / s[:, None])
    n_re = bf(NOISE * rn(R, L))
    n_im = bf(NOISE * rn(R, L))
    gain = bf(np.exp(SPREAD * rn(R)))
    return {"h_re": h_re, "h_im": h_im, "x_re": x_re, "x_im": x_im,
            "n_re": n_re, "n_im": n_im, "gain": gain}


def reference(h_re, h_im, x_re, x_im, n_re, n_im, gain):
    hr = mxq(f64(h_re), 1, "e4m3")
    hi = mxq(f64(h_im), 1, "e4m3")
    xr = mxq(f64(x_re), 0, "e4m3")
    xi = mxq(f64(x_im), 0, "e4m3")
    g = f64(gain)[:, None]
    y_re = g * ((hr @ xr) - (hi @ xi) + f64(n_re))
    y_im = g * ((hr @ xi) + (hi @ xr) + f64(n_im))
    y = np.stack([y_re, y_im], axis=1)
    Y = y.reshape(R, -1)
    words, scales = planes(Y)
    return y, words, scales

@@ -1,0 +1,283 @@
+from contextlib import ExitStack
+
+import concourse.mybir as mybir
+from concourse.masks import make_identity
+
+R, T, L = 1536, 1024, 512
+FLOPS = 4 * 2 * R * T * L
+
+F32 = mybir.dt.float32
+BF16 = mybir.dt.bfloat16
+U32 = mybir.dt.uint32
+I32 = mybir.dt.int32
+U8 = mybir.dt.uint8
+FP8X4 = mybir.dt.float8_e4m3fn_x4
+ALU = mybir.AluOpType
+COPY = mybir.ActivationFunctionType.Copy
+
+P = 128
+PACK = 4
+K_PASS = P * PACK
+PASSES = T // K_PASS
+GROUPS = R // K_PASS
+RE, IM = 0, 1
+CHUNK = 256
+RUN = 4
+LAST_VECTOR_COLS = 160
+NOISE_AHEAD = 5
+
+
+def tile_mimo_received_block_g2_kernel(tc, h_re, h_im, x_re, x_im, n_re, n_im, gain, out_0, out_1, out_2):
+    nc = tc.nc
+    h_in = (h_re, h_im)
+    x_in = (x_re, x_im)
+    n_in = (n_re, n_im)
+
+    with ExitStack() as ctx:
+        keep = ctx.enter_context(tc.tile_pool(name="keep", bufs=1))
+        work = ctx.enter_context(tc.tile_pool(name="work", bufs=1))
+        psum = ctx.enter_context(tc.psum_pool(name="psum", bufs=1))
+        ctx.enter_context(tc.manual_schedule())
+
+        h_raw, x_raw, n_raw = {}, {}, {}
+        x_grouped, x_codes, x_scales = {}, {}, {}
+        h_bank, h_grouped, h_codes, h_scales = {}, {}, {}, {}
+        acc, noise, y, y_grouped, y_codes, y_scales = {}, {}, {}, {}, {}, {}
+
+        def load_x(part, kp):
+            raw = keep.tile([P, PACK, L], BF16, name="x_raw_%d_%d" % (part, kp))
+            rows = x_in[part][kp * K_PASS : (kp + 1) * K_PASS, :]
+            nc.sync.dma_start(out=raw[:], in_=rows.rearrange("(p j) l -> p j l", j=PACK))
+            x_raw[part, kp] = raw
+
+        def load_h(unit, count):
+            g, t = divmod(unit, PACK)
+            for part in (RE, IM):
+                raw = keep.tile([P, count, T], BF16, name="h_raw_%d_%d" % (part, unit))
+                rows = h_in[part][g * K_PASS : (g + 1) * K_PASS, :].rearrange("(p j) k -> p j k", j=PACK)
+                nc.sync.dma_start(out=raw[:], in_=rows[:, t : t + count, :])
+                for i in range(count):
+                    h_raw[part, unit + i] = raw[:, i, :]
+
+        def load_n(part, g):
+            raw = keep.tile([P, PACK, L], BF16, name="n_raw_%d_%d" % (part, g))
+            rows = n_in[part][g * K_PASS : (g + 1) * K_PASS, :]
+            nc.sync.dma_start(out=raw[:], in_=rows.rearrange("(p j) l -> p j l", j=PACK))
+            n_raw[part, g] = raw
+
+        def interleave(copy, dst, src):
+            copy(
+                out=dst.rearrange("p (c i) t -> p c t i", i=RUN),
+                in_=src.rearrange("p t (c i) -> p c t i", i=RUN),
+            )
+
+        def group_x(copy, part, kp):
+            grouped = work.tile([P, L, PACK], BF16, name="x_grouped", bufs=4, align_bytes=64)
+            interleave(copy, grouped[:], x_raw[part, kp][:])
+            x_grouped[part, kp] = grouped[:].rearrange("p l t -> p (l t)")
+
+        def negate_x_im(kp):
+            negated = work.tile([P, L * PACK], BF16, name="x_negated", bufs=2, align_bytes=64)
+            nc.vector.tensor_scalar(out=negated[:], in0=x_grouped[IM, kp], scalar1=-1.0, scalar2=None, op0=ALU.mult)
+            x_grouped["neg", kp] = negated[:]
+
+        def quantize_x(key, kp):
+            codes = keep.tile([P, L], U32, name="x_codes_%s_%d" % (key, kp), align_bytes=64)
+            scales = keep.tile([P, L], U8, name="x_scales_%s_%d" % (key, kp), align_bytes=64)
+            nc.vector.quantize_mx(out=codes[:].bitcast(FP8X4), scales=scales[:], in_=x_grouped[key, kp])
+            x_codes[key, kp], x_scales[key, kp] = codes, scales
+
+        def transpose_h(unit):
+            for part in (RE, IM):
+                bank = psum.tile([P, PASSES, 2, P], F32, name="h_bank", bufs=4)
+                words = h_raw[part, unit].bitcast(F32)
+                for kp in range(PASSES):
+                    for half in range(2):
+                        first = kp * (K_PASS // 2) + half
+                        nc.tensor.transpose(bank[:, kp, half, :], words[:, first : (kp + 1) * (K_PASS // 2) : 2], ident[:])
+                h_bank[part, unit] = bank
+
+        def group_h(unit):
+            grouped = work.tile([P, 2 * PASSES * P * PACK], BF16, name="h_grouped", bufs=3, align_bytes=64)
+            words = grouped[:].bitcast(F32).rearrange("p (a k r h) -> p a k r h", a=2, k=PASSES, h=2)
+            for part in (RE, IM):
+                nc.scalar.copy(out=words[:, part], in_=h_bank[part, unit][:].rearrange("p k h r -> p k r h"))
+            h_grouped[unit] = grouped
+
+        def quantize_h(unit):
+            codes = work.tile([P, 2 * PASSES * P], U32, name="h_codes", bufs=8, align_bytes=64)
+            scales = work.tile([P, 2 * PASSES * P], U8, name="h_scales", bufs=8, align_bytes=64)
+            nc.vector.quantize_mx(out=codes[:].bitcast(FP8X4), scales=scales[:], in_=h_grouped[unit][:])
+            h_codes[unit], h_scales[unit] = codes, scales
+
+        def multiply(job, kps):
+            g, part, t, col, width = job
+            unit = g * PACK + t
+            if kps[0] == 0:
+                acc[job] = psum.tile([P, L], F32, name="acc", bufs=4)
+            terms = ((RE, RE), (IM, "neg")) if part == RE else ((IM, RE), (RE, IM))
+            for kp in kps:
+                for i, (h_part, x_key) in enumerate(terms):
+                    rows = slice((h_part * PASSES + kp) * P, (h_part * PASSES + kp + 1) * P)
+                    nc.tensor.matmul_mx(
+                        out=acc[job][:, :width],
+                        lhsT=h_codes[unit][:, rows].bitcast(FP8X4),
+                        lhsT_scale=h_scales[unit][:, rows],
+                        rhs=x_codes[x_key, kp][:, col : col + width].bitcast(FP8X4),
+                        rhs_scale=x_scales[x_key, kp][:, col : col + width],
+                        start=(kp == 0 and i == 0),
+                        stop=(kp == PASSES - 1 and i == 1),
+                    )
+
+        def scale_noise(g, part, t):
+            scaled = work.tile([P, L], F32, name="noise", bufs=NOISE_AHEAD + 4)
+            unit = g * PACK + t
+            nc.scalar.activation(out=scaled[:], in_=n_raw[part, g][:, t, :], func=COPY, scale=gain_f32[:, unit : unit + 1])
+            noise[g, part, t] = scaled
+
+        def finish(job):
+            g, part, t, col, width = job
+            unit = g * PACK + t
+            if (g, part) not in y:
+                y[g, part] = work.tile([P, PACK, L], F32, name="y", bufs=4)
+            nc.vector.scalar_tensor_tensor(
+                out=y[g, part][:, t, col : col + width],
+                in0=acc[job][:, :width],
+                scalar=gain_f32[:, unit : unit + 1],
+                in1=noise[g, part, t][:, col : col + width],
+                op0=ALU.mult,
+                op1=ALU.add,
+            )
+
+        def store_y(g, part, t0, t1, col, width):
+            rows = out_0[g * K_PASS : (g + 1) * K_PASS, part, col : col + width].rearrange("(p j) l -> p j l", j=PACK)
+            nc.sync.dma_start(out=rows[:, t0:t1, :], in_=y[g, part][:, t0:t1, col : col + width])
+
+        def group_y(copy, g, part, col, first=0, last=CHUNK):
+            if (g, part, col) not in y_grouped:
+                y_grouped[g, part, col] = work.tile([P, CHUNK, PACK], BF16, name="y_grouped", bufs=4, align_bytes=64)
+            interleave(copy, y_grouped[g, part, col][:, first:last, :], y[g, part][:, :, col + first : col + last])
+
+        def quantize_y(g, part, col):
+            if g not in y_codes:
+                y_codes[g] = keep.tile([P, 2 * L], U32, name="y_codes_%d" % g, align_bytes=64)
+                y_scales[g] = keep.tile([P, 2 * L], U8, name="y_scales_%d" % g, align_bytes=64)
+            cols = slice(part * L + col, part * L + col + CHUNK)
+            nc.vector.quantize_mx(
+                out=y_codes[g][:, cols].bitcast(FP8X4),
+                scales=y_scales[g][:, cols],
+                in_=y_grouped[g, part, col][:].rearrange("p l t -> p (l t)"),
+            )
+
+        def store_words(g, first, last):
+            words = out_1[g].rearrange("p m t -> p (m t)").bitcast(I32)
+            nc.sync.dma_start(out=words[:, first:last], in_=y_codes[g][:, first:last].bitcast(I32))
+
+        def store_scales(g, queues):
+            for q in range(4):
+                queues[q % 2].dma_start(
+                    out=out_2[g, 4 * q : 4 * q + 4, :].bitcast(I32),
+                    in_=y_scales[g][32 * q : 32 * q + 4, :].bitcast(I32),
+                )
+
+        gain_raw = keep.tile([P, GROUPS, PACK], BF16)
+        nc.scalar.dma_start(out=gain_raw[:], in_=gain.rearrange("(g p j) -> p g j", p=P, j=PACK))
+        ident = keep.tile([P, P], F32)
+        make_identity(nc, ident[:])
+
+        load_x(RE, 0)
+        load_h(0, 1)
+        load_x(IM, 0)
+        load_x(RE, 1)
+        load_x(IM, 1)
+        for unit in (1, 2, 3):
+            load_h(unit, 1)
+        for half in range(2 * GROUPS):
+            load_n(IM if half % 2 == 0 else RE, half // 2)
+            if half < 4:
+                load_h(4 + 2 * half, 2)
+
+        gain_f32 = keep.tile([P, GROUPS * PACK], F32)
+        nc.scalar.activation(out=gain_f32[:], in_=gain_raw[:].rearrange("p g j -> p (g j)"), func=COPY)
+
+        last = GROUPS - 1
+        jobs = [(g, part, t, 0, L) for g in range(GROUPS) for part in (IM, RE) for t in range(PACK)][:-PACK]
+        whole = len(jobs)
+        jobs = jobs + [(last, RE, t, col, CHUNK) for col in (0, CHUNK) for t in range(PACK)]
+        noise_jobs = [job[:3] for job in jobs if job[3] == 0]
+
+        group_x(nc.vector.tensor_copy, RE, 0)
+        transpose_h(0)
+        group_h(0)
+        quantize_x(RE, 0)
+        group_x(nc.vector.tensor_copy, IM, 0)
+        quantize_h(0)
+        quantize_x(IM, 0)
+        multiply(jobs[0], [0])
+        group_x(nc.scalar.copy, RE, 1)
+        group_x(nc.vector.tensor_copy, IM, 1)
+        transpose_h(1)
+        group_h(1)
+        quantize_x(RE, 1)
+        quantize_x(IM, 1)
+        multiply(jobs[0], [1])
+        transpose_h(2)
+        group_h(2)
+        quantize_h(1)
+        negate_x_im(0)
+        quantize_h(2)
+        quantize_x("neg", 0)
+        negate_x_im(1)
+
+        noise_done = [0]
+        for b in range(1, len(jobs) + 1):
+            unit = (b + 5) // 2 if b % 2 == 1 and b <= 17 else None
+            if unit is not None:
+                transpose_h(unit)
+                group_h(unit)
+            if b < len(jobs):
+                multiply(jobs[b], [0, 1])
+            while noise_done[0] < min(len(noise_jobs), b + 2 + min(NOISE_AHEAD, max(0, b - 6) // 2)):
+                scale_noise(*noise_jobs[noise_done[0]])
+                noise_done[0] = noise_done[0] + 1
+            g, part, t, col, width = jobs[b - 1]
+            if b == 1:
+                quantize_x("neg", 1)
+            finish(jobs[b - 1])
+            if b > len(jobs) - PACK:
+                store_y(g, part, t, t + 1, col, width)
+            elif t % 2 == 1:
+                store_y(g, part, t - 1, t + 1, col, width)
+            if b >= PACK:
+                done, step = divmod(b - PACK, PACK)
+                dg, dpart, dt, dcol, dwidth = jobs[done * PACK]
+                if done < 4:
+                    if step < 2:
+                        group_y(nc.vector.tensor_copy, dg, dpart, step * CHUNK)
+                    if step in (1, 2):
+                        quantize_y(dg, dpart, (step - 1) * CHUNK)
+                    if step == 2 and dpart == RE:
+                        store_words(dg, 0, 2 * L)
+                        store_scales(dg, (nc.sync, nc.sync))
+                elif done == 4:
+                    if step < 2:
+                        group_y(nc.scalar.copy, dg, dpart, step * CHUNK)
+                    if step == 3:
+                        quantize_y(dg, dpart, 0)
+                elif done == 5:
+                    if step == 0:
+                        group_y(nc.scalar.copy, dg, dpart, 0)
+                        quantize_y(dg, IM, CHUNK)
+                        store_words(dg, L, 2 * L)
+                    if step == 3:
+                        quantize_y(dg, dpart, 0)
+                        store_words(dg, 0, CHUNK)
+                else:
+                    group_y(nc.scalar.copy, dg, dpart, dcol, LAST_VECTOR_COLS, CHUNK)
+                    group_y(nc.vector.tensor_copy, dg, dpart, dcol, 0, LAST_VECTOR_COLS)
+            if unit is not None:
+                quantize_h(unit)
+
+        quantize_y(last, RE, CHUNK)
+        store_words(last, CHUNK, L)
+        store_scales(last, (nc.scalar, nc.sync))

@@ -23,8 +23,20 @@ GROUPS = R // K_PASS
 RE, IM = 0, 1
 CHUNK = 256
 RUN = 4
+FINE_FROM = 16
+X3 = 272
+Y_S_FROM = 99
+AHEAD_FROM = 14
+SORT_FROM = 5
+X2 = 352
 LAST_VECTOR_COLS = 160
 NOISE_AHEAD = 5
+RAW_SLOTS = 14
+X_VECTOR_COLS = 336
+WARM = 3
+SORT_S = 1
+SORT_V = 1
+T_AT = 3
 
 
 def tile_mimo_received_block_g2_kernel(tc, h_re, h_im, x_re, x_im, n_re, n_im, gain, out_0, out_1, out_2):
@@ -41,11 +53,11 @@ def tile_mimo_received_block_g2_kernel(tc, h_re, h_im, x_re, x_im, n_re, n_im, g
 
         h_raw, x_raw, n_raw = {}, {}, {}
         x_grouped, x_codes, x_scales = {}, {}, {}
-        h_bank, h_grouped, h_codes, h_scales = {}, {}, {}, {}
+        h_sorted, h_bank, h_grouped, h_codes, h_scales = {}, {}, {}, {}, {}
         acc, noise, y, y_grouped, y_codes, y_scales = {}, {}, {}, {}, {}, {}
 
         def load_x(part, kp):
-            raw = keep.tile([P, PACK, L], BF16, name="x_raw_%d_%d" % (part, kp))
+            raw = work.tile([P, PACK, L], BF16, name="x_raw", tag="raw", bufs=RAW_SLOTS)
             rows = x_in[part][kp * K_PASS : (kp + 1) * K_PASS, :]
             nc.sync.dma_start(out=raw[:], in_=rows.rearrange("(p j) l -> p j l", j=PACK))
             x_raw[part, kp] = raw
@@ -53,14 +65,17 @@ def tile_mimo_received_block_g2_kernel(tc, h_re, h_im, x_re, x_im, n_re, n_im, g
         def load_h(unit, count):
             g, t = divmod(unit, PACK)
             for part in (RE, IM):
-                raw = keep.tile([P, count, T], BF16, name="h_raw_%d_%d" % (part, unit))
+                if count == 1:
+                    raw = keep.tile([P, count, T], BF16, name="h_raw_%d_%d" % (part, unit))
+                else:
+                    raw = work.tile([P, count, T], BF16, name="h_raw", tag="raw", bufs=RAW_SLOTS)
                 rows = h_in[part][g * K_PASS : (g + 1) * K_PASS, :].rearrange("(p j) k -> p j k", j=PACK)
                 nc.sync.dma_start(out=raw[:], in_=rows[:, t : t + count, :])
                 for i in range(count):
                     h_raw[part, unit + i] = raw[:, i, :]
 
         def load_n(part, g):
-            raw = keep.tile([P, PACK, L], BF16, name="n_raw_%d_%d" % (part, g))
+            raw = work.tile([P, PACK, L], BF16, name="n_raw", tag="raw", bufs=RAW_SLOTS)
             rows = n_in[part][g * K_PASS : (g + 1) * K_PASS, :]
             nc.sync.dma_start(out=raw[:], in_=rows.rearrange("(p j) l -> p j l", j=PACK))
             n_raw[part, g] = raw
@@ -71,10 +86,35 @@ def tile_mimo_received_block_g2_kernel(tc, h_re, h_im, x_re, x_im, n_re, n_im, g
                 in_=src.rearrange("p t (c i) -> p c t i", i=RUN),
             )
 
-        def group_x(copy, part, kp):
+        def group_x(part, kp, split):
             grouped = work.tile([P, L, PACK], BF16, name="x_grouped", bufs=4, align_bytes=64)
-            interleave(copy, grouped[:], x_raw[part, kp][:])
+            if split < L:
+                interleave(nc.scalar.copy, grouped[:, split:, :], x_raw[part, kp][:, :, split:])
+            if split > 0:
+                interleave(nc.vector.tensor_copy, grouped[:, :split, :], x_raw[part, kp][:, :, :split])
             x_grouped[part, kp] = grouped[:].rearrange("p l t -> p (l t)")
+
+        def sort_h(copy, part, unit):
+            ordered = work.tile([P, 2, PASSES * P], F32, name="h_sorted", bufs=4)
+            words = h_raw[part, unit].bitcast(F32)
+            copy(
+                out=ordered[:].rearrange("p h (c i) -> p c h i", i=RUN),
+                in_=words.rearrange("p (c i h) -> p c h i", i=RUN, h=2),
+            )
+            h_sorted[part, unit] = ordered
+
+        def warm_up(count):
+            scratch = psum.tile([P, L], F32, name="acc", bufs=4)
+            for i in range(count):
+                nc.tensor.matmul_mx(
+                    out=scratch[:],
+                    lhsT=x_codes[RE, 0][:, :P].bitcast(FP8X4),
+                    lhsT_scale=x_scales[RE, 0][:, :P],
+                    rhs=x_codes[RE, 0][:].bitcast(FP8X4),
+                    rhs_scale=x_scales[RE, 0][:],
+                    start=True,
+                    stop=True,
+                )
 
         def negate_x_im(kp):
             negated = work.tile([P, L * PACK], BF16, name="x_negated", bufs=2, align_bytes=64)
@@ -94,15 +134,19 @@ def tile_mimo_received_block_g2_kernel(tc, h_re, h_im, x_re, x_im, n_re, n_im, g
                 for kp in range(PASSES):
                     for half in range(2):
                         first = kp * (K_PASS // 2) + half
-                        nc.tensor.transpose(bank[:, kp, half, :], words[:, first : (kp + 1) * (K_PASS // 2) : 2], ident[:])
+                        if (part, unit) in h_sorted:
+                            source = h_sorted[part, unit][:, half, kp * P : (kp + 1) * P]
+                        else:
+                            source = words[:, first : (kp + 1) * (K_PASS // 2) : 2]
+                        nc.tensor.transpose(bank[:, kp, half, :], source, ident[:])
                 h_bank[part, unit] = bank
 
-        def group_h(unit):
-            grouped = work.tile([P, 2 * PASSES * P * PACK], BF16, name="h_grouped", bufs=3, align_bytes=64)
-            words = grouped[:].bitcast(F32).rearrange("p (a k r h) -> p a k r h", a=2, k=PASSES, h=2)
-            for part in (RE, IM):
+        def group_h(unit, parts=(RE, IM)):
+            if unit not in h_grouped:
+                h_grouped[unit] = work.tile([P, 2 * PASSES * P * PACK], BF16, name="h_grouped", bufs=3, align_bytes=64)
+            words = h_grouped[unit][:].bitcast(F32).rearrange("p (a k r h) -> p a k r h", a=2, k=PASSES, h=2)
+            for part in parts:
                 nc.scalar.copy(out=words[:, part], in_=h_bank[part, unit][:].rearrange("p k h r -> p k r h"))
-            h_grouped[unit] = grouped
 
         def quantize_h(unit):
             codes = work.tile([P, 2 * PASSES * P], U32, name="h_codes", bufs=8, align_bytes=64)
@@ -110,14 +154,15 @@ def tile_mimo_received_block_g2_kernel(tc, h_re, h_im, x_re, x_im, n_re, n_im, g
             nc.vector.quantize_mx(out=codes[:].bitcast(FP8X4), scales=scales[:], in_=h_grouped[unit][:])
             h_codes[unit], h_scales[unit] = codes, scales
 
-        def multiply(job, kps):
+        def multiply(job, kps, only=(0, 1)):
             g, part, t, col, width = job
             unit = g * PACK + t
-            if kps[0] == 0:
+            if job not in acc:
                 acc[job] = psum.tile([P, L], F32, name="acc", bufs=4)
             terms = ((RE, RE), (IM, "neg")) if part == RE else ((IM, RE), (RE, IM))
             for kp in kps:
-                for i, (h_part, x_key) in enumerate(terms):
+                for i in only:
+                    h_part, x_key = terms[i]
                     rows = slice((h_part * PASSES + kp) * P, (h_part * PASSES + kp + 1) * P)
                     nc.tensor.matmul_mx(
                         out=acc[job][:, :width],
@@ -161,11 +206,12 @@ def tile_mimo_received_block_g2_kernel(tc, h_re, h_im, x_re, x_im, n_re, n_im, g
         def quantize_y(g, part, col):
             if g not in y_codes:
                 y_codes[g] = keep.tile([P, 2 * L], U32, name="y_codes_%d" % g, align_bytes=64)
-                y_scales[g] = keep.tile([P, 2 * L], U8, name="y_scales_%d" % g, align_bytes=64)
+                if g < 2:
+                    y_scales[g] = keep.tile([P, 2 * L], U8, name="y_scales_%d" % g, align_bytes=64)
             cols = slice(part * L + col, part * L + col + CHUNK)
             nc.vector.quantize_mx(
                 out=y_codes[g][:, cols].bitcast(FP8X4),
-                scales=y_scales[g][:, cols],
+                scales=y_scales[g][:, cols] if g < 2 else y_scales[1][4:, cols],
                 in_=y_grouped[g, part, col][:].rearrange("p l t -> p (l t)"),
             )
 
@@ -173,11 +219,11 @@ def tile_mimo_received_block_g2_kernel(tc, h_re, h_im, x_re, x_im, n_re, n_im, g
             words = out_1[g].rearrange("p m t -> p (m t)").bitcast(I32)
             nc.sync.dma_start(out=words[:, first:last], in_=y_codes[g][:, first:last].bitcast(I32))
 
-        def store_scales(g, queues):
+        def store_scales(first, count, queues):
             for q in range(4):
                 queues[q % 2].dma_start(
-                    out=out_2[g, 4 * q : 4 * q + 4, :].bitcast(I32),
-                    in_=y_scales[g][32 * q : 32 * q + 4, :].bitcast(I32),
+                    out=out_2[first : first + count, 4 * q : 4 * q + 4, :].bitcast(I32),
+                    in_=y_scales[first][32 * q : 32 * q + 4 * count, :].bitcast(I32),
                 )
 
         gain_raw = keep.tile([P, GROUPS, PACK], BF16)
@@ -188,14 +234,26 @@ def tile_mimo_received_block_g2_kernel(tc, h_re, h_im, x_re, x_im, n_re, n_im, g
         load_x(RE, 0)
         load_h(0, 1)
         load_x(IM, 0)
+        load_h(1, 1)
         load_x(RE, 1)
         load_x(IM, 1)
-        for unit in (1, 2, 3):
-            load_h(unit, 1)
+        load_h(2, 1)
+        load_n(IM, 0)
+        load_h(3, 1)
+        stream = []
         for half in range(2 * GROUPS):
-            load_n(IM if half % 2 == 0 else RE, half // 2)
+            stream.append(("n", IM if half % 2 == 0 else RE, half // 2))
             if half < 4:
-                load_h(4 + 2 * half, 2)
+                stream.append(("h", 4 + 2 * half, 2))
+
+        def load_stream(items):
+            for kind, first, second in items:
+                if kind == "n":
+                    load_n(first, second)
+                else:
+                    load_h(first, second)
+
+        load_stream(stream[1:7])
 
         gain_f32 = keep.tile([P, GROUPS * PACK], F32)
         nc.scalar.activation(out=gain_f32[:], in_=gain_raw[:].rearrange("p g j -> p (g j)"), func=COPY)
@@ -206,78 +264,93 @@ def tile_mimo_received_block_g2_kernel(tc, h_re, h_im, x_re, x_im, n_re, n_im, g
         jobs = jobs + [(last, RE, t, col, CHUNK) for col in (0, CHUNK) for t in range(PACK)]
         noise_jobs = [job[:3] for job in jobs if job[3] == 0]
 
-        group_x(nc.vector.tensor_copy, RE, 0)
+        group_x(RE, 0, X_VECTOR_COLS)
         transpose_h(0)
-        group_h(0)
         quantize_x(RE, 0)
-        group_x(nc.vector.tensor_copy, IM, 0)
-        quantize_h(0)
+        warm_up(WARM)
+        group_h(0, [RE])
+        group_x(IM, 0, X2)
+        group_h(0, [IM])
         quantize_x(IM, 0)
-        multiply(jobs[0], [0])
-        group_x(nc.scalar.copy, RE, 1)
-        group_x(nc.vector.tensor_copy, IM, 1)
+        quantize_h(0)
+        group_x(RE, 1, X2)
         transpose_h(1)
         group_h(1)
+        multiply(jobs[0], [0])
         quantize_x(RE, 1)
+        multiply(jobs[0], [1], [0])
+        quantize_h(1)
+        group_x(IM, 1, X3)
         quantize_x(IM, 1)
-        multiply(jobs[0], [1])
         transpose_h(2)
         group_h(2)
-        quantize_h(1)
-        negate_x_im(0)
+        multiply(jobs[1], [0])
+        multiply(jobs[1], [1], [0])
+        multiply(jobs[0], [1], [1])
+        multiply(jobs[1], [1], [1])
         quantize_h(2)
-        quantize_x("neg", 0)
-        negate_x_im(1)
+        negate_x_im(0)
 
+        load_stream(stream[7:])
         noise_done = [0]
         for b in range(1, len(jobs) + 1):
-            unit = (b + 5) // 2 if b % 2 == 1 and b <= 17 else None
+            unit = 3 if b == 2 else (b + 5) // 2 if b % 2 == 1 and 3 <= b <= 17 else None
+            to_sort = (b + 7) // 2 if b % 2 == 1 and SORT_FROM <= (b + 7) // 2 < 12 else None
             if unit is not None:
                 transpose_h(unit)
                 group_h(unit)
-            if b < len(jobs):
+            if 1 < b < len(jobs):
                 multiply(jobs[b], [0, 1])
-            while noise_done[0] < min(len(noise_jobs), b + 2 + min(NOISE_AHEAD, max(0, b - 6) // 2)):
+            if to_sort is not None and SORT_S:
+                sort_h(nc.scalar.copy, RE, to_sort)
+            while noise_done[0] < min(len(noise_jobs), b + 1 + (b > 1) + (0 if b < 17 else 2 * (b - 16))):
                 scale_noise(*noise_jobs[noise_done[0]])
                 noise_done[0] = noise_done[0] + 1
             g, part, t, col, width = jobs[b - 1]
-            if b == 1:
+            if b == 2:
+                negate_x_im(1)
+                quantize_h(unit)
                 quantize_x("neg", 1)
+                unit = None
             finish(jobs[b - 1])
-            if b > len(jobs) - PACK:
+            if b == 1:
+                quantize_x("neg", 0)
+            if b > len(jobs) - PACK or FINE_FROM < b <= whole:
                 store_y(g, part, t, t + 1, col, width)
             elif t % 2 == 1:
                 store_y(g, part, t - 1, t + 1, col, width)
-            if b >= PACK:
-                done, step = divmod(b - PACK, PACK)
-                dg, dpart, dt, dcol, dwidth = jobs[done * PACK]
-                if done < 4:
-                    if step < 2:
-                        group_y(nc.vector.tensor_copy, dg, dpart, step * CHUNK)
-                    if step in (1, 2):
-                        quantize_y(dg, dpart, (step - 1) * CHUNK)
-                    if step == 2 and dpart == RE:
-                        store_words(dg, 0, 2 * L)
-                        store_scales(dg, (nc.sync, nc.sync))
-                elif done == 4:
-                    if step < 2:
-                        group_y(nc.scalar.copy, dg, dpart, step * CHUNK)
-                    if step == 3:
-                        quantize_y(dg, dpart, 0)
-                elif done == 5:
-                    if step == 0:
-                        group_y(nc.scalar.copy, dg, dpart, 0)
-                        quantize_y(dg, IM, CHUNK)
-                        store_words(dg, L, 2 * L)
-                    if step == 3:
-                        quantize_y(dg, dpart, 0)
-                        store_words(dg, 0, CHUNK)
+            if to_sort is not None and SORT_V:
+                sort_h(nc.vector.tensor_copy, IM, to_sort)
+            if PACK < b <= whole:
+                done, step = divmod(b - PACK - 1, PACK)
+                dg, dpart = jobs[done * PACK][:2]
+                if step % 2 == 0:
+                    group_y(nc.vector.tensor_copy if b < Y_S_FROM else nc.scalar.copy, dg, dpart, step // 2 * CHUNK)
                 else:
-                    group_y(nc.scalar.copy, dg, dpart, dcol, LAST_VECTOR_COLS, CHUNK)
-                    group_y(nc.vector.tensor_copy, dg, dpart, dcol, 0, LAST_VECTOR_COLS)
+                    quantize_y(dg, dpart, step // 2 * CHUNK)
+                if step == 3:
+                    store_words(dg, dpart * L, (dpart + 1) * L)
+                    if done == 1:
+                        store_scales(0, 1, (nc.sync, nc.sync))
+            if b == whole:
+                group_y(nc.scalar.copy, last, IM, 0)
+            if b == whole + 1:
+                group_y(nc.scalar.copy, last, IM, CHUNK)
+            if b == whole + 3:
+                quantize_y(last, IM, 0)
+            if b == whole + 4:
+                group_y(nc.scalar.copy, last, RE, 0)
+            if b == whole + 5:
+                quantize_y(last, IM, CHUNK)
+                store_words(last, L, 2 * L)
+            if b == whole + 8:
+                quantize_y(last, RE, 0)
+                store_words(last, 0, CHUNK)
+                group_y(nc.scalar.copy, last, RE, CHUNK, LAST_VECTOR_COLS, CHUNK)
+                group_y(nc.vector.tensor_copy, last, RE, CHUNK, 0, LAST_VECTOR_COLS)
             if unit is not None:
                 quantize_h(unit)
 
         quantize_y(last, RE, CHUNK)
         store_words(last, CHUNK, L)
-        store_scales(last, (nc.scalar, nc.sync))
+        store_scales(1, 2, (nc.scalar, nc.sync))

from contextlib import ExitStack

import concourse.mybir as mybir
from concourse.masks import make_identity

R, T, L = 1536, 1024, 512
FLOPS = 4 * 2 * R * T * L

F32 = mybir.dt.float32
BF16 = mybir.dt.bfloat16
U32 = mybir.dt.uint32
I32 = mybir.dt.int32
U8 = mybir.dt.uint8
FP8X4 = mybir.dt.float8_e4m3fn_x4
ALU = mybir.AluOpType
COPY = mybir.ActivationFunctionType.Copy

P = 128
PACK = 4
K_PASS = P * PACK
PASSES = T // K_PASS
GROUPS = R // K_PASS
RE, IM = 0, 1
CHUNK = 256
RUN = 4
FINE_FROM = 16
X3 = 272
Y_S_FROM = 99
AHEAD_FROM = 14
SORT_FROM = 5
X2 = 352
LAST_VECTOR_COLS = 160
NOISE_AHEAD = 5
RAW_SLOTS = 14
X_VECTOR_COLS = 336
WARM = 3
SORT_S = 1
SORT_V = 1
T_AT = 3


def tile_mimo_received_block_g2_kernel(tc, h_re, h_im, x_re, x_im, n_re, n_im, gain, out_0, out_1, out_2):
    nc = tc.nc
    h_in = (h_re, h_im)
    x_in = (x_re, x_im)
    n_in = (n_re, n_im)

    with ExitStack() as ctx:
        keep = ctx.enter_context(tc.tile_pool(name="keep", bufs=1))
        work = ctx.enter_context(tc.tile_pool(name="work", bufs=1))
        psum = ctx.enter_context(tc.psum_pool(name="psum", bufs=1))
        ctx.enter_context(tc.manual_schedule())

        h_raw, x_raw, n_raw = {}, {}, {}
        x_grouped, x_codes, x_scales = {}, {}, {}
        h_sorted, h_bank, h_grouped, h_codes, h_scales = {}, {}, {}, {}, {}
        acc, noise, y, y_grouped, y_codes, y_scales = {}, {}, {}, {}, {}, {}

        def load_x(part, kp):
            raw = work.tile([P, PACK, L], BF16, name="x_raw", tag="raw", bufs=RAW_SLOTS)
            rows = x_in[part][kp * K_PASS : (kp + 1) * K_PASS, :]
            nc.sync.dma_start(out=raw[:], in_=rows.rearrange("(p j) l -> p j l", j=PACK))
            x_raw[part, kp] = raw

        def load_h(unit, count):
            g, t = divmod(unit, PACK)
            for part in (RE, IM):
                if count == 1:
                    raw = keep.tile([P, count, T], BF16, name="h_raw_%d_%d" % (part, unit))
                else:
                    raw = work.tile([P, count, T], BF16, name="h_raw", tag="raw", bufs=RAW_SLOTS)
                rows = h_in[part][g * K_PASS : (g + 1) * K_PASS, :].rearrange("(p j) k -> p j k", j=PACK)
                nc.sync.dma_start(out=raw[:], in_=rows[:, t : t + count, :])
                for i in range(count):
                    h_raw[part, unit + i] = raw[:, i, :]

        def load_n(part, g):
            raw = work.tile([P, PACK, L], BF16, name="n_raw", tag="raw", bufs=RAW_SLOTS)
            rows = n_in[part][g * K_PASS : (g + 1) * K_PASS, :]
            nc.sync.dma_start(out=raw[:], in_=rows.rearrange("(p j) l -> p j l", j=PACK))
            n_raw[part, g] = raw

        def interleave(copy, dst, src):
            copy(
                out=dst.rearrange("p (c i) t -> p c t i", i=RUN),
                in_=src.rearrange("p t (c i) -> p c t i", i=RUN),
            )

        def group_x(part, kp, split):
            grouped = work.tile([P, L, PACK], BF16, name="x_grouped", bufs=4, align_bytes=64)
            if split < L:
                interleave(nc.scalar.copy, grouped[:, split:, :], x_raw[part, kp][:, :, split:])
            if split > 0:
                interleave(nc.vector.tensor_copy, grouped[:, :split, :], x_raw[part, kp][:, :, :split])
            x_grouped[part, kp] = grouped[:].rearrange("p l t -> p (l t)")

        def sort_h(copy, part, unit):
            ordered = work.tile([P, 2, PASSES * P], F32, name="h_sorted", bufs=4)
            words = h_raw[part, unit].bitcast(F32)
            copy(
                out=ordered[:].rearrange("p h (c i) -> p c h i", i=RUN),
                in_=words.rearrange("p (c i h) -> p c h i", i=RUN, h=2),
            )
            h_sorted[part, unit] = ordered

        def warm_up(count):
            scratch = psum.tile([P, L], F32, name="acc", bufs=4)
            for i in range(count):
                nc.tensor.matmul_mx(
                    out=scratch[:],
                    lhsT=x_codes[RE, 0][:, :P].bitcast(FP8X4),
                    lhsT_scale=x_scales[RE, 0][:, :P],
                    rhs=x_codes[RE, 0][:].bitcast(FP8X4),
                    rhs_scale=x_scales[RE, 0][:],
                    start=True,
                    stop=True,
                )

        def negate_x_im(kp):
            negated = work.tile([P, L * PACK], BF16, name="x_negated", bufs=2, align_bytes=64)
            nc.vector.tensor_scalar(out=negated[:], in0=x_grouped[IM, kp], scalar1=-1.0, scalar2=None, op0=ALU.mult)
            x_grouped["neg", kp] = negated[:]

        def quantize_x(key, kp):
            codes = keep.tile([P, L], U32, name="x_codes_%s_%d" % (key, kp), align_bytes=64)
            scales = keep.tile([P, L], U8, name="x_scales_%s_%d" % (key, kp), align_bytes=64)
            nc.vector.quantize_mx(out=codes[:].bitcast(FP8X4), scales=scales[:], in_=x_grouped[key, kp])
            x_codes[key, kp], x_scales[key, kp] = codes, scales

        def transpose_h(unit):
            for part in (RE, IM):
                bank = psum.tile([P, PASSES, 2, P], F32, name="h_bank", bufs=4)
                words = h_raw[part, unit].bitcast(F32)
                for kp in range(PASSES):
                    for half in range(2):
                        first = kp * (K_PASS // 2) + half
                        if (part, unit) in h_sorted:
                            source = h_sorted[part, unit][:, half, kp * P : (kp + 1) * P]
                        else:
                            source = words[:, first : (kp + 1) * (K_PASS // 2) : 2]
                        nc.tensor.transpose(bank[:, kp, half, :], source, ident[:])
                h_bank[part, unit] = bank

        def group_h(unit, parts=(RE, IM)):
            if unit not in h_grouped:
                h_grouped[unit] = work.tile([P, 2 * PASSES * P * PACK], BF16, name="h_grouped", bufs=3, align_bytes=64)
            words = h_grouped[unit][:].bitcast(F32).rearrange("p (a k r h) -> p a k r h", a=2, k=PASSES, h=2)
            for part in parts:
                nc.scalar.copy(out=words[:, part], in_=h_bank[part, unit][:].rearrange("p k h r -> p k r h"))

        def quantize_h(unit):
            codes = work.tile([P, 2 * PASSES * P], U32, name="h_codes", bufs=8, align_bytes=64)
            scales = work.tile([P, 2 * PASSES * P], U8, name="h_scales", bufs=8, align_bytes=64)
            nc.vector.quantize_mx(out=codes[:].bitcast(FP8X4), scales=scales[:], in_=h_grouped[unit][:])
            h_codes[unit], h_scales[unit] = codes, scales

        def multiply(job, kps, only=(0, 1)):
            g, part, t, col, width = job
            unit = g * PACK + t
            if job not in acc:
                acc[job] = psum.tile([P, L], F32, name="acc", bufs=4)
            terms = ((RE, RE), (IM, "neg")) if part == RE else ((IM, RE), (RE, IM))
            for kp in kps:
                for i in only:
                    h_part, x_key = terms[i]
                    rows = slice((h_part * PASSES + kp) * P, (h_part * PASSES + kp + 1) * P)
                    nc.tensor.matmul_mx(
                        out=acc[job][:, :width],
                        lhsT=h_codes[unit][:, rows].bitcast(FP8X4),
                        lhsT_scale=h_scales[unit][:, rows],
                        rhs=x_codes[x_key, kp][:, col : col + width].bitcast(FP8X4),
                        rhs_scale=x_scales[x_key, kp][:, col : col + width],
                        start=(kp == 0 and i == 0),
                        stop=(kp == PASSES - 1 and i == 1),
                    )

        def scale_noise(g, part, t):
            scaled = work.tile([P, L], F32, name="noise", bufs=NOISE_AHEAD + 4)
            unit = g * PACK + t
            nc.scalar.activation(out=scaled[:], in_=n_raw[part, g][:, t, :], func=COPY, scale=gain_f32[:, unit : unit + 1])
            noise[g, part, t] = scaled

        def finish(job):
            g, part, t, col, width = job
            unit = g * PACK + t
            if (g, part) not in y:
                y[g, part] = work.tile([P, PACK, L], F32, name="y", bufs=4)
            nc.vector.scalar_tensor_tensor(
                out=y[g, part][:, t, col : col + width],
                in0=acc[job][:, :width],
                scalar=gain_f32[:, unit : unit + 1],
                in1=noise[g, part, t][:, col : col + width],
                op0=ALU.mult,
                op1=ALU.add,
            )

        def store_y(g, part, t0, t1, col, width):
            rows = out_0[g * K_PASS : (g + 1) * K_PASS, part, col : col + width].rearrange("(p j) l -> p j l", j=PACK)
            nc.sync.dma_start(out=rows[:, t0:t1, :], in_=y[g, part][:, t0:t1, col : col + width])

        def group_y(copy, g, part, col, first=0, last=CHUNK):
            if (g, part, col) not in y_grouped:
                y_grouped[g, part, col] = work.tile([P, CHUNK, PACK], BF16, name="y_grouped", bufs=4, align_bytes=64)
            interleave(copy, y_grouped[g, part, col][:, first:last, :], y[g, part][:, :, col + first : col + last])

        def quantize_y(g, part, col):
            if g not in y_codes:
                y_codes[g] = keep.tile([P, 2 * L], U32, name="y_codes_%d" % g, align_bytes=64)
                if g < 2:
                    y_scales[g] = keep.tile([P, 2 * L], U8, name="y_scales_%d" % g, align_bytes=64)
            cols = slice(part * L + col, part * L + col + CHUNK)
            nc.vector.quantize_mx(
                out=y_codes[g][:, cols].bitcast(FP8X4),
                scales=y_scales[g][:, cols] if g < 2 else y_scales[1][4:, cols],
                in_=y_grouped[g, part, col][:].rearrange("p l t -> p (l t)"),
            )

        def store_words(g, first, last):
            words = out_1[g].rearrange("p m t -> p (m t)").bitcast(I32)
            nc.sync.dma_start(out=words[:, first:last], in_=y_codes[g][:, first:last].bitcast(I32))

        def store_scales(first, count, queues):
            for q in range(4):
                queues[q % 2].dma_start(
                    out=out_2[first : first + count, 4 * q : 4 * q + 4, :].bitcast(I32),
                    in_=y_scales[first][32 * q : 32 * q + 4 * count, :].bitcast(I32),
                )

        gain_raw = keep.tile([P, GROUPS, PACK], BF16)
        nc.scalar.dma_start(out=gain_raw[:], in_=gain.rearrange("(g p j) -> p g j", p=P, j=PACK))
        ident = keep.tile([P, P], F32)
        make_identity(nc, ident[:])

        load_x(RE, 0)
        load_h(0, 1)
        load_x(IM, 0)
        load_h(1, 1)
        load_x(RE, 1)
        load_x(IM, 1)
        load_h(2, 1)
        load_n(IM, 0)
        load_h(3, 1)
        stream = []
        for half in range(2 * GROUPS):
            stream.append(("n", IM if half % 2 == 0 else RE, half // 2))
            if half < 4:
                stream.append(("h", 4 + 2 * half, 2))

        def load_stream(items):
            for kind, first, second in items:
                if kind == "n":
                    load_n(first, second)
                else:
                    load_h(first, second)

        load_stream(stream[1:7])

        gain_f32 = keep.tile([P, GROUPS * PACK], F32)
        nc.scalar.activation(out=gain_f32[:], in_=gain_raw[:].rearrange("p g j -> p (g j)"), func=COPY)

        last = GROUPS - 1
        jobs = [(g, part, t, 0, L) for g in range(GROUPS) for part in (IM, RE) for t in range(PACK)][:-PACK]
        whole = len(jobs)
        jobs = jobs + [(last, RE, t, col, CHUNK) for col in (0, CHUNK) for t in range(PACK)]
        noise_jobs = [job[:3] for job in jobs if job[3] == 0]

        group_x(RE, 0, X_VECTOR_COLS)
        transpose_h(0)
        quantize_x(RE, 0)
        warm_up(WARM)
        group_h(0, [RE])
        group_x(IM, 0, X2)
        group_h(0, [IM])
        quantize_x(IM, 0)
        quantize_h(0)
        group_x(RE, 1, X2)
        transpose_h(1)
        group_h(1)
        multiply(jobs[0], [0])
        quantize_x(RE, 1)
        multiply(jobs[0], [1], [0])
        quantize_h(1)
        group_x(IM, 1, X3)
        quantize_x(IM, 1)
        transpose_h(2)
        group_h(2)
        multiply(jobs[1], [0])
        multiply(jobs[1], [1], [0])
        multiply(jobs[0], [1], [1])
        multiply(jobs[1], [1], [1])
        quantize_h(2)
        negate_x_im(0)

        load_stream(stream[7:])
        noise_done = [0]
        for b in range(1, len(jobs) + 1):
            unit = 3 if b == 2 else (b + 5) // 2 if b % 2 == 1 and 3 <= b <= 17 else None
            to_sort = (b + 7) // 2 if b % 2 == 1 and SORT_FROM <= (b + 7) // 2 < 12 else None
            if unit is not None:
                transpose_h(unit)
                group_h(unit)
            if 1 < b < len(jobs):
                multiply(jobs[b], [0, 1])
            if to_sort is not None and SORT_S:
                sort_h(nc.scalar.copy, RE, to_sort)
            while noise_done[0] < min(len(noise_jobs), b + 1 + (b > 1) + (0 if b < 17 else 2 * (b - 16))):
                scale_noise(*noise_jobs[noise_done[0]])
                noise_done[0] = noise_done[0] + 1
            g, part, t, col, width = jobs[b - 1]
            if b == 2:
                negate_x_im(1)
                quantize_h(unit)
                quantize_x("neg", 1)
                unit = None
            finish(jobs[b - 1])
            if b == 1:
                quantize_x("neg", 0)
            if b > len(jobs) - PACK or FINE_FROM < b <= whole:
                store_y(g, part, t, t + 1, col, width)
            elif t % 2 == 1:
                store_y(g, part, t - 1, t + 1, col, width)
            if to_sort is not None and SORT_V:
                sort_h(nc.vector.tensor_copy, IM, to_sort)
            if PACK < b <= whole:
                done, step = divmod(b - PACK - 1, PACK)
                dg, dpart = jobs[done * PACK][:2]
                if step % 2 == 0:
                    group_y(nc.vector.tensor_copy if b < Y_S_FROM else nc.scalar.copy, dg, dpart, step // 2 * CHUNK)
                else:
                    quantize_y(dg, dpart, step // 2 * CHUNK)
                if step == 3:
                    store_words(dg, dpart * L, (dpart + 1) * L)
                    if done == 1:
                        store_scales(0, 1, (nc.sync, nc.sync))
            if b == whole:
                group_y(nc.scalar.copy, last, IM, 0)
            if b == whole + 1:
                group_y(nc.scalar.copy, last, IM, CHUNK)
            if b == whole + 3:
                quantize_y(last, IM, 0)
            if b == whole + 4:
                group_y(nc.scalar.copy, last, RE, 0)
            if b == whole + 5:
                quantize_y(last, IM, CHUNK)
                store_words(last, L, 2 * L)
            if b == whole + 8:
                quantize_y(last, RE, 0)
                store_words(last, 0, CHUNK)
                group_y(nc.scalar.copy, last, RE, CHUNK, LAST_VECTOR_COLS, CHUNK)
                group_y(nc.vector.tensor_copy, last, RE, CHUNK, 0, LAST_VECTOR_COLS)
            if unit is not None:
                quantize_h(unit)

        quantize_y(last, RE, CHUNK)
        store_words(last, CHUNK, L)
        store_scales(1, 2, (nc.scalar, nc.sync))
